import numpy as np
import ml_dtypes

BF16 = ml_dtypes.bfloat16


def bf(x):
    return np.asarray(x, np.float32).astype(BF16)


def f32(x):
    return np.asarray(x, np.float32)


def f64(x):
    return np.asarray(x).astype(np.float64)


def striped(idx):
    return np.tile(idx.reshape(-1, 16).T, (8, 1))


def rows(idx, k):
    return np.tile(idx, (k, 1))


def look(tab, idx):
    return np.take_along_axis(f64(tab), rows(idx, len(tab)), axis=1)


K, S, V, N = 128, 4096, 2048, 2048


def setup_inputs():
    return {"tab": f32(np.random.standard_normal((2, K, S))), "offs": striped(np.random.permutation(S)[:N])}


def reference(tab, offs):
    idx = offs[:16].T.reshape(-1)
    x = 1.0 / (1.0 + np.exp(-look(tab[0], idx))) * np.tanh(look(tab[1], idx))
    return x

@@ -1,0 +1,34 @@
+import concourse.mybir as mybir
+
+F32 = mybir.dt.float32
+U16 = mybir.dt.uint16
+SIGMOID = mybir.ActivationFunctionType.Sigmoid
+TANH = mybir.ActivationFunctionType.Tanh
+MULT = mybir.AluOpType.mult
+
+LIST_ROWS = 16
+PIECE = 512
+
+
+def tile_lookup_cell_sigtanh_out_kernel(tc, tab, offs, out):
+    nc = tc.nc
+    rows, places = tab.shape[1], tab.shape[2]
+    picked = out.shape[1]
+    with tc.tile_pool(name="held", bufs=1) as held:
+        offsets = held.tile([rows, picked // LIST_ROWS], U16, name="offsets")
+        gate_table = held.tile([rows, places], F32, name="gate_table")
+        state_table = held.tile([rows, places], F32, name="state_table")
+        gate = held.tile([rows, picked], F32, name="gate")
+        nc.sync.dma_start(offsets[:], offs)
+        nc.sync.dma_start(gate_table[:], tab[0])
+        nc.sync.dma_start(state_table[:], tab[1])
+
+        nc.scalar.activation(gate[:], gate_table[:].indirect(offsets[:]), SIGMOID)
+        for first in range(0, picked, PIECE):
+            last = first + PIECE
+            piece_offsets = offsets[:, first // LIST_ROWS : last // LIST_ROWS]
+            state = held.tile([rows, PIECE], F32, name=f"state_{first}")
+            product = held.tile([rows, PIECE], F32, name=f"product_{first}")
+            nc.scalar.activation(state[:], state_table[:].indirect(piece_offsets), TANH)
+            nc.vector.tensor_tensor(product[:], gate[:, first:last], state[:], MULT)
+            nc.sync.dma_start(out[:, first:last], product[:])

@@ -7,7 +7,7 @@ TANH = mybir.ActivationFunctionType.Tanh
 MULT = mybir.AluOpType.mult
 
 LIST_ROWS = 16
-PIECE = 512
+PIECE = 256
 
 
 def tile_lookup_cell_sigtanh_out_kernel(tc, tab, offs, out):
@@ -23,12 +23,17 @@ def tile_lookup_cell_sigtanh_out_kernel(tc, tab, offs, out):
         nc.sync.dma_start(gate_table[:], tab[0])
         nc.sync.dma_start(state_table[:], tab[1])
 
+        warm_in = held.tile([rows, 1], F32, name="warm_in")
+        warm_out = held.tile([rows, 1], F32, name="warm_out")
+        nc.vector.memset(warm_in[:], 0.0)
+        nc.scalar.activation(warm_out[:], warm_in[:], SIGMOID)
+
         nc.scalar.activation(gate[:], gate_table[:].indirect(offsets[:]), SIGMOID)
-        for first in range(0, picked, PIECE):
-            last = first + PIECE
+        cuts = list(range(0, picked, PIECE)) + [picked - PIECE // 2, picked]
+        for first, last in zip(cuts, cuts[1:]):
             piece_offsets = offsets[:, first // LIST_ROWS : last // LIST_ROWS]
-            state = held.tile([rows, PIECE], F32, name=f"state_{first}")
-            product = held.tile([rows, PIECE], F32, name=f"product_{first}")
+            state = held.tile([rows, last - first], F32, name=f"state_{first}")
+            product = held.tile([rows, last - first], F32, name=f"product_{first}")
             nc.scalar.activation(state[:], state_table[:].indirect(piece_offsets), TANH)
             nc.vector.tensor_tensor(product[:], gate[:, first:last], state[:], MULT)
             nc.sync.dma_start(out[:, first:last], product[:])

@@ -7,7 +7,8 @@ TANH = mybir.ActivationFunctionType.Tanh
 MULT = mybir.AluOpType.mult
 
 LIST_ROWS = 16
-PIECE = 256
+PIECES = 5
+STEP = 128
 
 
 def tile_lookup_cell_sigtanh_out_kernel(tc, tab, offs, out):
@@ -29,7 +30,7 @@ def tile_lookup_cell_sigtanh_out_kernel(tc, tab, offs, out):
         nc.scalar.activation(warm_out[:], warm_in[:], SIGMOID)
 
         nc.scalar.activation(gate[:], gate_table[:].indirect(offsets[:]), SIGMOID)
-        cuts = list(range(0, picked, PIECE)) + [picked - PIECE // 2, picked]
+        cuts = [0] + [picked - STEP * k * (k + 1) // 2 for k in reversed(range(PIECES))]
         for first, last in zip(cuts, cuts[1:]):
             piece_offsets = offsets[:, first // LIST_ROWS : last // LIST_ROWS]
             state = held.tile([rows, last - first], F32, name=f"state_{first}")

import concourse.mybir as mybir

F32 = mybir.dt.float32
U16 = mybir.dt.uint16
SIGMOID = mybir.ActivationFunctionType.Sigmoid
TANH = mybir.ActivationFunctionType.Tanh
MULT = mybir.AluOpType.mult

LIST_ROWS = 16
PIECES = 5
STEP = 128


def tile_lookup_cell_sigtanh_out_kernel(tc, tab, offs, out):
    nc = tc.nc
    rows, places = tab.shape[1], tab.shape[2]
    picked = out.shape[1]
    with tc.tile_pool(name="held", bufs=1) as held:
        offsets = held.tile([rows, picked // LIST_ROWS], U16, name="offsets")
        gate_table = held.tile([rows, places], F32, name="gate_table")
        state_table = held.tile([rows, places], F32, name="state_table")
        gate = held.tile([rows, picked], F32, name="gate")
        nc.sync.dma_start(offsets[:], offs)
        nc.sync.dma_start(gate_table[:], tab[0])
        nc.sync.dma_start(state_table[:], tab[1])

        warm_in = held.tile([rows, 1], F32, name="warm_in")
        warm_out = held.tile([rows, 1], F32, name="warm_out")
        nc.vector.memset(warm_in[:], 0.0)
        nc.scalar.activation(warm_out[:], warm_in[:], SIGMOID)

        nc.scalar.activation(gate[:], gate_table[:].indirect(offsets[:]), SIGMOID)
        cuts = [0] + [picked - STEP * k * (k + 1) // 2 for k in reversed(range(PIECES))]
        for first, last in zip(cuts, cuts[1:]):
            piece_offsets = offsets[:, first // LIST_ROWS : last // LIST_ROWS]
            state = held.tile([rows, last - first], F32, name=f"state_{first}")
            product = held.tile([rows, last - first], F32, name=f"product_{first}")
            nc.scalar.activation(state[:], state_table[:].indirect(piece_offsets), TANH)
            nc.vector.tensor_tensor(product[:], gate[:, first:last], state[:], MULT)
            nc.sync.dma_start(out[:, first:last], product[:])
